import numpy as np
import ml_dtypes


def mxq(x, axis, fmt="e4m3"):
    dtype, down = {"e4m3": (ml_dtypes.float8_e4m3fn, 7), "e5m2": (ml_dtypes.float8_e5m2, 14)}[fmt]
    v = np.moveaxis(np.asarray(x, np.float32).astype(ml_dtypes.bfloat16).astype(np.float64), axis, -1)
    blocks = v.reshape(v.shape[:-1] + (-1, 32))
    amax = np.abs(blocks).max(-1, keepdims=True)
    byte = np.maximum(np.where(amax > 0, np.frexp(amax)[1] - 1 + 127, 0) - down, 1)
    scale = np.exp2(byte - 127.0)
    codes = (blocks / scale).astype(np.float32).astype(dtype).astype(np.float64)
    return np.moveaxis((codes * scale).reshape(v.shape), -1, axis)


WIDE = False


def mx_kscale(k):
    if not WIDE:
        return np.ones(k)
    levels = np.array([30, -30])
    if k % 512:
        return np.exp2(np.random.permutation(np.resize(levels, k // 32))).repeat(32)
    a = np.empty((k // 512, 16))
    for p in range(k // 512):
        a[p, :8] = np.random.permutation(np.resize(levels, 8))
        for g in range(8):
            far = levels[np.abs(levels - a[p, g]) >= 10]
            a[p, g + 8] = far[np.random.randint(len(far))]
    return np.exp2(a.ravel()).repeat(32)


def f64(x):
    return np.asarray(x).astype(np.float64)


def striped(idx):
    return np.tile(np.asarray(idx).reshape(-1, 16).T, (8, 1)).astype(np.uint16)


def unstriped(offs):
    return offs[:16].T.reshape(-1).astype(np.int64)


def striped8(idx):
    return np.asarray(idx).reshape(8, -1, 16).transpose(0, 2, 1).reshape(128, -1).astype(np.uint16)


def unstriped8(offs):
    return offs.reshape(8, 16, -1).transpose(0, 2, 1).reshape(8, -1).astype(np.int64)


def pick8(x, idx, run):
    r = np.arange(len(x))
    return x[r[:, None], idx[r % (8 * run) // run]]


E2M1 = np.array([0.0, 0.5, 1.0, 1.5, 2.0, 3.0, 4.0, 6.0, -0.0, -0.5, -1.0, -1.5, -2.0, -3.0, -4.0, -6.0])


def pack_weight(w, fmt):
    k, n = w.shape
    w = f64(np.asarray(w, np.float32).astype(ml_dtypes.bfloat16)).reshape(k // 32, 32, n)
    amax = np.abs(w).max(1)
    if fmt in ("e4m3", "e5m2"):
        byte = np.frexp(amax)[1] - 1 + 127 - (7 if fmt == "e4m3" else 14)
    else:
        mant, ex = np.frexp(amax / 6.0)
        byte = np.where(mant > 0.5, ex, ex - 1) + 127
    byte = np.clip(np.where(amax > 0, byte, 1), 1, 254)
    scaled = (w * np.exp2(127.0 - byte)[:, None, :]).reshape(k, n).astype(np.float32)
    by_word = np.ascontiguousarray(scaled.reshape(k // 512, 128, 4, n).transpose(0, 1, 3, 2))
    if fmt in ("e4m3", "e5m2"):
        words = by_word.astype(ml_dtypes.float8_e4m3fn if fmt == "e4m3" else ml_dtypes.float8_e5m2).view(np.uint8)
    else:
        c = by_word.astype(ml_dtypes.float4_e2m1fn).view(np.uint8) & 0xF
        words = (c[..., 0::2] | (c[..., 1::2] << 4)).reshape(k // 512, 128, 2 * n)
    return np.ascontiguousarray(words), np.ascontiguousarray(byte.astype(np.uint8).reshape(k // 512, 16, n))


def unpack_weight(words, scales, fmt):
    g, _, n = scales.shape
    words = np.ascontiguousarray(words).reshape(g, 128, n, -1)
    if fmt in ("e4m3", "e5m2"):
        vals = words.view(ml_dtypes.float8_e4m3fn if fmt == "e4m3" else ml_dtypes.float8_e5m2).astype(np.float64)
    else:
        nib = np.empty((g, 128, n, 4), np.uint8)
        nib[..., 0::2] = words & 0xF
        nib[..., 1::2] = words >> 4
        vals = E2M1[nib]
    vals = vals * np.repeat(np.exp2(scales.astype(np.float64) - 127.0), 8, axis=1)[..., None]
    return vals.transpose(0, 1, 3, 2).reshape(g * 512, n)


K, T, J, R, O, U, D, N, S, E = 512, 2048, 256, 512, 128, 128, 256, 256, 1024, 512


def setup_inputs():
    n = np.random.standard_normal
    idx = np.random.permutation(T)[:J]
    idx2 = np.random.permutation(T)[:J]
    idx3 = np.stack([np.random.permutation(J)[:O] for _ in range(8)])
    idx4 = np.stack([np.random.permutation(J)[:U] for _ in range(8)])
    idx5 = np.random.permutation(S)[:N]
    idx6 = np.random.permutation(E)[:D]
    idx7 = np.random.permutation(E)[:D]
    fk = mx_kscale(K)
    fr = mx_kscale(R)
    xtp = pack_weight(n((K, T)) / fk[:, None], "e4m3")
    wp = pack_weight(n((K, R)) * 1 / np.sqrt(K) * fk[:, None] * fr, "e2m1")
    w2p = pack_weight(n((K, R)) * 1 / np.sqrt(K) * fk[:, None], "e5m2")
    vsp = pack_weight(n((R, S)) * 1 / np.sqrt(R) / fr[:, None], "e5m2")
    return {
        "xt_words": xtp[0],
        "xt_scales": xtp[1],
        "w_words": wp[0],
        "w_scales": wp[1],
        "w2_words": w2p[0],
        "w2_scales": w2p[1],
        "vs_words": vsp[0],
        "vs_scales": vsp[1],
        "offs": striped(idx),
        "offs2": striped(idx2),
        "offs3": striped8(idx3),
        "offs4": striped8(idx4),
        "offs5": striped(idx5),
        "offs6": striped(idx6),
        "offs7": striped(idx7),
    }


def reference(xt_words, xt_scales, w_words, w_scales, w2_words, w2_scales, vs_words, vs_scales, offs, offs2, offs3, offs4, offs5, offs6, offs7):
    idx = unstriped(offs)
    idx2 = unstriped(offs2)
    idx3 = unstriped8(offs3)
    idx4 = unstriped8(offs4)
    idx5 = unstriped(offs5)
    idx6 = unstriped(offs6)
    idx7 = unstriped(offs7)
    xtu = unpack_weight(xt_words, xt_scales, "e4m3")
    wu = unpack_weight(w_words, w_scales, "e2m1")
    w2u = unpack_weight(w2_words, w2_scales, "e5m2")
    vsu = unpack_weight(vs_words, vs_scales, "e5m2")
    xtidxg = xtu[:, idx]
    a = wu.T @ xtidxg
    xtidx2g = xtu[:, idx2]
    b = w2u.T @ xtidx2g
    lb = b[:, 0:1]
    la = a[:, 0:1]
    h1 = pick8(a, idx3, 64) * lb
    h2 = pick8(b, idx4, 64) * la
    hid = np.concatenate([h1, h2], axis=1)
    vsidx5g = vsu[:, idx5]
    hidq = mxq(hid, 0, "e4m3")
    p = vsidx5g.T @ hidq
    pa = np.zeros((N, E))
    pa[:, idx6] = p
    pb = np.zeros((N, E))
    pb[:, idx7] = p
    y = pa + pb
    return y

@@ -1,0 +1,201 @@
+from contextlib import ExitStack
+
+import concourse.mybir as mybir
+
+K, T, J, R, O, D, N, S, E = 512, 2048, 256, 512, 128, 256, 256, 1024, 512
+FLOPS = 2 * K * R * J * 2 + 2 * R * N * D
+
+F32 = mybir.dt.float32
+BF16 = mybir.dt.bfloat16
+I32 = mybir.dt.int32
+U32 = mybir.dt.uint32
+U16 = mybir.dt.uint16
+U8 = mybir.dt.uint8
+E4M3 = mybir.dt.float8_e4m3fn_x4
+E5M2 = mybir.dt.float8_e5m2_x4
+E2M1 = mybir.dt.float4_e2m1fn_x4
+COPY = mybir.ActivationFunctionType.Copy
+ADD = mybir.AluOpType.add
+
+P = 128
+PACK = 4
+QUADS = 4
+
+
+def tile_list_groupside_ahead_store_pagetwice_kernel(
+    tc, xt_words, xt_scales, w_words, w_scales, w2_words, w2_scales, vs_words, vs_scales,
+    offs, offs2, offs3, offs4, offs5, offs6, offs7, out,
+):
+    nc = tc.nc
+    with ExitStack() as ctx:
+        sb = ctx.enter_context(tc.tile_pool(name="sb", bufs=1))
+        psum = ctx.enter_context(tc.psum_pool(name="psum", bufs=8))
+
+        def load_list(src, name):
+            lst = sb.tile(list(src.shape), U16, name=name)
+            nc.sync.dma_start(lst[:], src)
+            return lst
+
+        def load_plane(plane, src):
+            for q in range(QUADS):
+                nc.sync.dma_start(plane[32 * q : 32 * q + 4, :].bitcast(I32), src[0, 4 * q : 4 * q + 4, :].bitcast(I32))
+
+        def words_of(src):
+            return src[0].rearrange("p n t -> p (n t)").bitcast(I32)
+
+        def stage_scales(src, name):
+            stage = sb.tile([4, QUADS, R // 4], I32, name=name)
+            nc.gpsimd.dma_start(stage[:], src[0].bitcast(I32).rearrange("(q r) c -> r q c", r=4))
+            return stage
+
+        def dealt_scales(stage, plane, name):
+            for q in range(QUADS):
+                nc.vector.tensor_copy(plane[32 * q : 32 * q + 4, :].bitcast(I32), stage[:, q, :])
+            dealt = sb.tile([P, PACK, P], U8, name=name, align_bytes=64)
+            nc.vector.tensor_copy(dealt[:].rearrange("p t m -> p m t"), plane[:].rearrange("p (m t) -> p m t", t=PACK))
+            return dealt
+
+        def dealt_words(raw, dtype, name):
+            dealt = sb.tile([P, PACK, P], dtype, name=name, align_bytes=64)
+            nc.scalar.copy(dealt[:].rearrange("p t m -> p m t"), raw[:].rearrange("p (m t) -> p m t", t=PACK))
+            return dealt
+
+        def gather(window, lst, dtype, name, tag=None):
+            picked = sb.tile([P, J], dtype, name=name, tag=tag or name, align_bytes=64)
+            nc.vector.tensor_copy(picked[:], window[:].indirect(lst[:]))
+            return picked
+
+        l1 = load_list(offs, "l1")
+        w_raw = sb.tile([P, R], U16, name="w_raw")
+        nc.scalar.dma_start(w_raw[:].bitcast(I32), w_words[0].bitcast(I32))
+        l2 = load_list(offs2, "l2")
+        xw = sb.tile([P, T], U32, name="xw")
+        nc.scalar.dma_start(xw[:].bitcast(I32), words_of(xt_words))
+        xs = sb.tile([P, T], U8, name="xs", tag="xt_bytes", align_bytes=64)
+        nc.vector.memset(xs[:].bitcast(I32), 0)
+        load_plane(xs, xt_scales)
+        ws_stage = stage_scales(w_scales, "ws_stage")
+        w2s_stage = stage_scales(w2_scales, "w2s_stage")
+        w2_raw = sb.tile([P, R], U32, name="w2_raw")
+        nc.sync.dma_start(w2_raw[:].bitcast(I32), words_of(w2_words))
+
+        ws_plane = sb.tile([P, R], U8, name="ws_plane")
+        w2s_plane = sb.tile([P, R], U8, name="w2s_plane")
+        vsc = sb.tile([P, S], U8, name="vsc", tag="vs_bytes", align_bytes=64)
+        for plane in (ws_plane, w2s_plane, vsc):
+            nc.vector.memset(plane[:].bitcast(I32), 0)
+        pa = [sb.tile([P, E], F32, name=f"pa{i}") for i in range(2)]
+        pb = [sb.tile([P, E], F32, name=f"pb{i}") for i in range(2)]
+        for page in pa + pb:
+            nc.vector.memset(page[:], 0.0)
+
+        l3 = load_list(offs3, "l3")
+        l4 = load_list(offs4, "l4")
+        vw = sb.tile([P, S], U32, name="vw", tag="vs_words", align_bytes=64)
+        nc.sync.dma_start(vw[:].bitcast(I32), words_of(vs_words))
+        load_plane(vsc, vs_scales)
+        l5 = load_list(offs5, "l5")
+        l6 = load_list(offs6, "l6")
+        l7 = load_list(offs7, "l7")
+
+        xs1 = gather(xs, l1, U8, "xs1")
+        xs2 = gather(xs, l2, U8, "xs2")
+        ws = dealt_scales(ws_stage, ws_plane, "ws")
+        w = dealt_words(w_raw, U16, "w")
+        xw1 = gather(xw, l1, U32, "xw1", tag="xt_bytes")
+        w2s = dealt_scales(w2s_stage, w2s_plane, "w2s")
+        w2 = dealt_words(w2_raw, U32, "w2")
+        xw2 = gather(xw, l2, U32, "xw2")
+
+        def product(words, fmt, scales, t, xwg, xsg):
+            acc = psum.tile([P, J], F32, name="acc", tag="acc")
+            nc.tensor.matmul_mx(
+                out=acc[:], lhsT=words[:, t, :].bitcast(fmt), lhsT_scale=scales[:, t, :],
+                rhs=xwg[:].bitcast(E4M3), rhs_scale=xsg[:], start=True, stop=True,
+            )
+            return acc
+
+        a = [sb.tile([P, J], F32, name=f"a{t}") for t in range(PACK)]
+        b = [sb.tile([P, J], F32, name=f"b{t}") for t in range(PACK)]
+        h = [sb.tile([P, PACK, O], BF16, name=f"h{i}") for i in range(2)]
+
+        def make_a(t):
+            acc = product(w, E2M1, ws, t, xw1, xs1)
+            if t < 2:
+                nc.scalar.copy(a[t][:], acc[:])
+            else:
+                nc.vector.tensor_copy(a[t][:], acc[:])
+
+        def make_b(t):
+            nc.vector.tensor_copy(b[t][:], product(w2, E5M2, w2s, t, xw2, xs2)[:])
+
+        def look(half, t):
+            src, lst, other = ((a, l3, b), (b, l4, a))[half]
+            nc.scalar.activation(out=h[half][:, t, :], in_=src[t][:].indirect(lst[:]), func=COPY, scale=other[t][:, 0:1])
+
+        make_a(0)
+        make_a(1)
+        make_b(0)
+        make_b(1)
+        look(0, 0)
+        look(0, 1)
+        make_a(2)
+        make_b(2)
+        look(1, 0)
+        look(0, 2)
+        make_a(3)
+        make_b(3)
+        look(1, 1)
+        look(0, 3)
+        look(1, 2)
+        look(1, 3)
+
+        vsg = gather(vsc, l5, U8, "vsg")
+        vwg = gather(vw, l5, U32, "vwg")
+
+        def second_stage(half):
+            woven = sb.tile([P, O, PACK], BF16, name=f"woven{half}", tag="vs_words", align_bytes=64)
+            nc.vector.tensor_copy(
+                woven[:].rearrange("p (c i) t -> p c t i", i=4), h[half][:].rearrange("p t (c i) -> p c t i", i=4)
+            )
+            codes = sb.tile([P, O], U32, name=f"codes{half}", tag=("vs_bytes", "codes1")[half], align_bytes=64)
+            scales = sb.tile([P, O], U8, name=f"scales{half}", align_bytes=64)
+            nc.vector.quantize_mx(out=codes[:].bitcast(E4M3), scales=scales[:], in_=woven[:].rearrange("p d t -> p (d t)"))
+            acc = psum.tile([P, 2, O], F32, name="acc", tag="acc")
+            for i in range(2):
+                cols = slice(P * i, P * (i + 1))
+                nc.tensor.matmul_mx(
+                    out=acc[:, i, :], lhsT=vwg[:, cols].bitcast(E5M2), lhsT_scale=vsg[:, cols],
+                    rhs=codes[:].bitcast(E4M3), rhs_scale=scales[:], start=True, stop=True,
+                )
+            return acc
+
+        p = [sb.tile([P, 2, O], F32, name=f"p{half}") for half in range(2)]
+
+        def put(engine, page, lst, i, first, count):
+            half, col = divmod(first, O)
+            window = page[i][:].indirect(lst[:, first // 16 : (first + count) // 16])
+            if engine == "vector":
+                nc.vector.tensor_copy(window, p[half][:, i, col : col + count])
+            else:
+                nc.scalar.activation(out=window, in_=p[half][:, i, col : col + count], func=COPY)
+
+        def finish(i):
+            y = sb.tile([P, E], F32, name=f"y{i}")
+            nc.vector.tensor_tensor(y[:], pa[i][:], pb[i][:], ADD)
+            nc.sync.dma_start(out[P * i : P * (i + 1), :], y[:])
+
+        nc.scalar.copy(p[0][:], second_stage(0)[:])
+        late = second_stage(1)
+        put("vector", pa, l6, 0, 0, O)
+        put("scalar", pb, l7, 0, 0, O)
+        nc.vector.tensor_copy(p[1][:], late[:])
+        put("vector", pa, l6, 1, 0, O)
+        put("scalar", pb, l7, 1, 0, O)
+        put("vector", pa, l6, 0, O, O)
+        put("scalar", pb, l7, 0, O, O)
+        put("vector", pa, l6, 1, O, O // 2)
+        put("scalar", pb, l7, 1, O, O)
+        finish(0)
+        put("scalar", pa, l6, 1, O + O // 2, O // 2)
+        finish(1)

@@ -43,9 +43,9 @@ def tile_list_groupside_ahead_store_pagetwice_kernel(
         def words_of(src):
             return src[0].rearrange("p n t -> p (n t)").bitcast(I32)
 
-        def stage_scales(src, name):
+        def stage_scales(queue, src, name):
             stage = sb.tile([4, QUADS, R // 4], I32, name=name)
-            nc.gpsimd.dma_start(stage[:], src[0].bitcast(I32).rearrange("(q r) c -> r q c", r=4))
+            queue.dma_start(stage[:], src[0].bitcast(I32).rearrange("(q r) c -> r q c", r=4))
             return stage
 
         def dealt_scales(stage, plane, name):
@@ -60,24 +60,24 @@ def tile_list_groupside_ahead_store_pagetwice_kernel(
             nc.scalar.copy(dealt[:].rearrange("p t m -> p m t"), raw[:].rearrange("p (m t) -> p m t", t=PACK))
             return dealt
 
-        def gather(window, lst, dtype, name, tag=None):
-            picked = sb.tile([P, J], dtype, name=name, tag=tag or name, align_bytes=64)
+        def gather(window, lst, dtype, name):
+            picked = sb.tile([P, J], dtype, name=name, align_bytes=64)
             nc.vector.tensor_copy(picked[:], window[:].indirect(lst[:]))
             return picked
 
-        l1 = load_list(offs, "l1")
-        w_raw = sb.tile([P, R], U16, name="w_raw")
-        nc.scalar.dma_start(w_raw[:].bitcast(I32), w_words[0].bitcast(I32))
         l2 = load_list(offs2, "l2")
+        w2s_stage = stage_scales(nc.scalar, w2_scales, "w2s_stage")
+        ws_stage = stage_scales(nc.sync, w_scales, "ws_stage")
         xw = sb.tile([P, T], U32, name="xw")
         nc.scalar.dma_start(xw[:].bitcast(I32), words_of(xt_words))
         xs = sb.tile([P, T], U8, name="xs", tag="xt_bytes", align_bytes=64)
-        nc.vector.memset(xs[:].bitcast(I32), 0)
+        nc.gpsimd.memset(xs[:].bitcast(I32), 0)
         load_plane(xs, xt_scales)
-        ws_stage = stage_scales(w_scales, "ws_stage")
-        w2s_stage = stage_scales(w2_scales, "w2s_stage")
+        l1 = load_list(offs, "l1")
         w2_raw = sb.tile([P, R], U32, name="w2_raw")
         nc.sync.dma_start(w2_raw[:].bitcast(I32), words_of(w2_words))
+        w_raw = sb.tile([P, R], U16, name="w_raw")
+        nc.sync.dma_start(w_raw[:].bitcast(I32), w_words[0].bitcast(I32))
 
         ws_plane = sb.tile([P, R], U8, name="ws_plane")
         w2s_plane = sb.tile([P, R], U8, name="w2s_plane")
@@ -98,55 +98,60 @@ def tile_list_groupside_ahead_store_pagetwice_kernel(
         l6 = load_list(offs6, "l6")
         l7 = load_list(offs7, "l7")
 
-        xs1 = gather(xs, l1, U8, "xs1")
-        xs2 = gather(xs, l2, U8, "xs2")
-        ws = dealt_scales(ws_stage, ws_plane, "ws")
-        w = dealt_words(w_raw, U16, "w")
-        xw1 = gather(xw, l1, U32, "xw1", tag="xt_bytes")
         w2s = dealt_scales(w2s_stage, w2s_plane, "w2s")
+        ws = dealt_scales(ws_stage, ws_plane, "ws")
+        xs2 = gather(xs, l2, U8, "xs2")
+        xs1 = gather(xs, l1, U8, "xs1")
         w2 = dealt_words(w2_raw, U32, "w2")
-        xw2 = gather(xw, l2, U32, "xw2")
+        w = dealt_words(w_raw, U16, "w")
+        HALF = J // 2
+        xw2 = sb.tile([P, J], U32, name="xw2", tag="xt_bytes", align_bytes=64)
 
-        def product(words, fmt, scales, t, xwg, xsg):
-            acc = psum.tile([P, J], F32, name="acc", tag="acc")
-            nc.tensor.matmul_mx(
-                out=acc[:], lhsT=words[:, t, :].bitcast(fmt), lhsT_scale=scales[:, t, :],
-                rhs=xwg[:].bitcast(E4M3), rhs_scale=xsg[:], start=True, stop=True,
+        def gather_xw2(part):
+            nc.vector.tensor_copy(
+                xw2[:, HALF * part : HALF * (part + 1)], xw[:].indirect(l2[:, HALF // 16 * part : HALF // 16 * (part + 1)])
             )
-            return acc
+
+        gather_xw2(0)
+        xw1 = gather(xw, l1, U32, "xw1")
+        gather_xw2(1)
 
         a = [sb.tile([P, J], F32, name=f"a{t}") for t in range(PACK)]
         b = [sb.tile([P, J], F32, name=f"b{t}") for t in range(PACK)]
         h = [sb.tile([P, PACK, O], BF16, name=f"h{i}") for i in range(2)]
 
         def make_a(t):
-            acc = product(w, E2M1, ws, t, xw1, xs1)
-            if t < 2:
-                nc.scalar.copy(a[t][:], acc[:])
-            else:
-                nc.vector.tensor_copy(a[t][:], acc[:])
+            acc = psum.tile([P, J], F32, name="acc", tag="acc")
+            nc.tensor.matmul_mx(
+                out=acc[:], lhsT=w[:, t, :].bitcast(E2M1), lhsT_scale=ws[:, t, :],
+                rhs=xw1[:].bitcast(E4M3), rhs_scale=xs1[:], start=True, stop=True,
+            )
+            nc.vector.tensor_copy(a[t][:], acc[:])
 
-        def make_b(t):
-            nc.vector.tensor_copy(b[t][:], product(w2, E5M2, w2s, t, xw2, xs2)[:])
+        def make_b(part, ts, copy):
+            cols = slice(HALF * part, HALF * (part + 1))
+            acc = psum.tile([P, len(ts), HALF], F32, name="acc", tag="acc")
+            for n, t in enumerate(ts):
+                nc.tensor.matmul_mx(
+                    out=acc[:, n, :], lhsT=w2[:, t, :].bitcast(E5M2), lhsT_scale=w2s[:, t, :],
+                    rhs=xw2[:, cols].bitcast(E4M3), rhs_scale=xs2[:, cols], start=True, stop=True,
+                )
+            for n, t in enumerate(ts):
+                copy(b[t][:, cols], acc[:, n, :])
 
         def look(half, t):
             src, lst, other = ((a, l3, b), (b, l4, a))[half]
             nc.scalar.activation(out=h[half][:, t, :], in_=src[t][:].indirect(lst[:]), func=COPY, scale=other[t][:, 0:1])
 
-        make_a(0)
-        make_a(1)
-        make_b(0)
-        make_b(1)
-        look(0, 0)
-        look(0, 1)
-        make_a(2)
-        make_b(2)
+        make_b(0, (0, 1), nc.scalar.copy)
+        make_b(0, (2, 3), nc.scalar.copy)
+        for t in range(PACK):
+            make_a(t)
+            look(0, t)
+        make_b(1, (0, 1), nc.vector.tensor_copy)
         look(1, 0)
-        look(0, 2)
-        make_a(3)
-        make_b(3)
         look(1, 1)
-        look(0, 3)
+        make_b(1, (2, 3), nc.scalar.copy)
         look(1, 2)
         look(1, 3)
 

@@ -20,6 +20,16 @@ ADD = mybir.AluOpType.add
 P = 128
 PACK = 4
 QUADS = 4
+QUAD_ROWS = P // QUADS
+SCALE_ROWS = 4
+ENTRIES = 16
+LINE = 16
+RUN = 4
+MX_ALIGN = 64
+PSUM_BANKS = 8
+SLOT_HALF = J // 2
+ROW_TILES = N // P
+PAGE_HALF = E // 2
 
 
 def tile_list_groupside_ahead_store_pagetwice_kernel(
@@ -29,39 +39,43 @@ def tile_list_groupside_ahead_store_pagetwice_kernel(
     nc = tc.nc
     with ExitStack() as ctx:
         sb = ctx.enter_context(tc.tile_pool(name="sb", bufs=1))
-        psum = ctx.enter_context(tc.psum_pool(name="psum", bufs=8))
+        psum = ctx.enter_context(tc.psum_pool(name="psum", bufs=PSUM_BANKS))
 
         def load_list(src, name):
             lst = sb.tile(list(src.shape), U16, name=name)
             nc.sync.dma_start(lst[:], src)
             return lst
 
+        def scale_rows(plane, q):
+            return plane[QUAD_ROWS * q : QUAD_ROWS * q + SCALE_ROWS, :].bitcast(I32)
+
         def load_plane(plane, src):
             for q in range(QUADS):
-                nc.sync.dma_start(plane[32 * q : 32 * q + 4, :].bitcast(I32), src[0, 4 * q : 4 * q + 4, :].bitcast(I32))
+                nc.sync.dma_start(scale_rows(plane, q), src[0, SCALE_ROWS * q : SCALE_ROWS * (q + 1), :].bitcast(I32))
 
         def words_of(src):
             return src[0].rearrange("p n t -> p (n t)").bitcast(I32)
 
         def stage_scales(queue, src, name):
-            stage = sb.tile([4, QUADS, R // 4], I32, name=name)
-            queue.dma_start(stage[:], src[0].bitcast(I32).rearrange("(q r) c -> r q c", r=4))
+            stage = sb.tile([SCALE_ROWS, QUADS, R // 4], I32, name=name)
+            queue.dma_start(stage[:], src[0].bitcast(I32).rearrange("(q i) c -> i q c", i=SCALE_ROWS))
             return stage
+
+        def deal(copy, raw, dtype, per_line, name):
+            dealt = sb.tile([P, PACK, P], dtype, name=name, align_bytes=MX_ALIGN)
+            copy(
+                dealt[:].rearrange("p t (c i) -> p c t i", i=per_line),
+                raw[:].rearrange("p (c i t) -> p c t i", i=per_line, t=PACK),
+            )
+            return dealt
 
         def dealt_scales(stage, plane, name):
             for q in range(QUADS):
-                nc.vector.tensor_copy(plane[32 * q : 32 * q + 4, :].bitcast(I32), stage[:, q, :])
-            dealt = sb.tile([P, PACK, P], U8, name=name, align_bytes=64)
-            nc.vector.tensor_copy(dealt[:].rearrange("p t m -> p m t"), plane[:].rearrange("p (m t) -> p m t", t=PACK))
-            return dealt
-
-        def dealt_words(raw, dtype, name):
-            dealt = sb.tile([P, PACK, P], dtype, name=name, align_bytes=64)
-            nc.scalar.copy(dealt[:].rearrange("p t m -> p m t"), raw[:].rearrange("p (m t) -> p m t", t=PACK))
-            return dealt
+                nc.vector.tensor_copy(scale_rows(plane, q), stage[:, q, :])
+            return deal(nc.vector.tensor_copy, plane, U8, LINE, name)
 
         def gather(window, lst, dtype, name):
-            picked = sb.tile([P, J], dtype, name=name, align_bytes=64)
+            picked = sb.tile([P, J], dtype, name=name, align_bytes=MX_ALIGN)
             nc.vector.tensor_copy(picked[:], window[:].indirect(lst[:]))
             return picked
 
@@ -70,7 +84,7 @@ def tile_list_groupside_ahead_store_pagetwice_kernel(
         ws_stage = stage_scales(nc.sync, w_scales, "ws_stage")
         xw = sb.tile([P, T], U32, name="xw")
         nc.scalar.dma_start(xw[:].bitcast(I32), words_of(xt_words))
-        xs = sb.tile([P, T], U8, name="xs", tag="xt_bytes", align_bytes=64)
+        xs = sb.tile([P, T], U8, name="xs", tag="xt_bytes", align_bytes=MX_ALIGN)
         nc.gpsimd.memset(xs[:].bitcast(I32), 0)
         load_plane(xs, xt_scales)
         l1 = load_list(offs, "l1")
@@ -81,20 +95,20 @@ def tile_list_groupside_ahead_store_pagetwice_kernel(
 
         ws_plane = sb.tile([P, R], U8, name="ws_plane")
         w2s_plane = sb.tile([P, R], U8, name="w2s_plane")
-        vsc = sb.tile([P, S], U8, name="vsc", tag="vs_bytes", align_bytes=64)
-        for plane in (ws_plane, w2s_plane, vsc):
+        vs_plane = sb.tile([P, S], U8, name="vs_plane", tag="vs_bytes", align_bytes=MX_ALIGN)
+        for plane in (ws_plane, w2s_plane, vs_plane):
             nc.vector.memset(plane[:].bitcast(I32), 0)
-        pa = [sb.tile([P, E], F32, name=f"pa{i}") for i in range(2)]
-        pb = [sb.tile([P, E], F32, name=f"pb{i}") for i in range(2)]
+        pa = [sb.tile([P, E], F32, name=f"pa{i}") for i in range(ROW_TILES)]
+        pb = [sb.tile([P, E], F32, name=f"pb{i}") for i in range(ROW_TILES)]
         for page in pa + pb:
             nc.vector.memset(page[:], 0.0)
 
+        vw = sb.tile([P, S], U32, name="vw", tag="vs_words", align_bytes=MX_ALIGN)
+        nc.sync.dma_start(vw[:].bitcast(I32), words_of(vs_words))
+        l5 = load_list(offs5, "l5")
         l3 = load_list(offs3, "l3")
         l4 = load_list(offs4, "l4")
-        vw = sb.tile([P, S], U32, name="vw", tag="vs_words", align_bytes=64)
-        nc.sync.dma_start(vw[:].bitcast(I32), words_of(vs_words))
-        load_plane(vsc, vs_scales)
-        l5 = load_list(offs5, "l5")
+        load_plane(vs_plane, vs_scales)
         l6 = load_list(offs6, "l6")
         l7 = load_list(offs7, "l7")
 
@@ -102,23 +116,24 @@ def tile_list_groupside_ahead_store_pagetwice_kernel(
         ws = dealt_scales(ws_stage, ws_plane, "ws")
         xs2 = gather(xs, l2, U8, "xs2")
         xs1 = gather(xs, l1, U8, "xs1")
-        w2 = dealt_words(w2_raw, U32, "w2")
-        w = dealt_words(w_raw, U16, "w")
-        HALF = J // 2
-        xw2 = sb.tile([P, J], U32, name="xw2", tag="xt_bytes", align_bytes=64)
+        w2 = deal(nc.scalar.copy, w2_raw, U32, LINE // 4, "w2")
+        w = deal(nc.scalar.copy, w_raw, U16, LINE // 2, "w")
+        xw2 = sb.tile([P, J], U32, name="xw2", tag="xt_bytes", align_bytes=MX_ALIGN)
 
         def gather_xw2(part):
-            nc.vector.tensor_copy(
-                xw2[:, HALF * part : HALF * (part + 1)], xw[:].indirect(l2[:, HALF // 16 * part : HALF // 16 * (part + 1)])
-            )
+            first, last = SLOT_HALF * part, SLOT_HALF * (part + 1)
+            nc.vector.tensor_copy(xw2[:, first:last], xw[:].indirect(l2[:, first // ENTRIES : last // ENTRIES]))
 
         gather_xw2(0)
         xw1 = gather(xw, l1, U32, "xw1")
         gather_xw2(1)
 
-        a = [sb.tile([P, J], F32, name=f"a{t}") for t in range(PACK)]
+        vwg = gather(vw, l5, U32, "vwg")
+        a = [
+            sb.tile([P, J], F32, name=f"a{t}", tag=f"a{t}" if t else "vs_words", align_bytes=MX_ALIGN) for t in range(PACK)
+        ]
         b = [sb.tile([P, J], F32, name=f"b{t}") for t in range(PACK)]
-        h = [sb.tile([P, PACK, O], BF16, name=f"h{i}") for i in range(2)]
+        hid = [sb.tile([P, PACK, O], BF16, name=f"hid{half}") for half in range(2)]
 
         def make_a(t):
             acc = psum.tile([P, J], F32, name="acc", tag="acc")
@@ -128,46 +143,44 @@ def tile_list_groupside_ahead_store_pagetwice_kernel(
             )
             nc.vector.tensor_copy(a[t][:], acc[:])
 
-        def make_b(part, ts, copy):
-            cols = slice(HALF * part, HALF * (part + 1))
-            acc = psum.tile([P, len(ts), HALF], F32, name="acc", tag="acc")
-            for n, t in enumerate(ts):
+        def make_b(part, pair, copy):
+            cols = slice(SLOT_HALF * part, SLOT_HALF * (part + 1))
+            acc = psum.tile([P, len(pair), SLOT_HALF], F32, name="acc", tag="acc")
+            for n, t in enumerate(pair):
                 nc.tensor.matmul_mx(
                     out=acc[:, n, :], lhsT=w2[:, t, :].bitcast(E5M2), lhsT_scale=w2s[:, t, :],
                     rhs=xw2[:, cols].bitcast(E4M3), rhs_scale=xs2[:, cols], start=True, stop=True,
                 )
-            for n, t in enumerate(ts):
+            for n, t in enumerate(pair):
                 copy(b[t][:, cols], acc[:, n, :])
 
-        def look(half, t):
+        def pick(half, t):
             src, lst, other = ((a, l3, b), (b, l4, a))[half]
-            nc.scalar.activation(out=h[half][:, t, :], in_=src[t][:].indirect(lst[:]), func=COPY, scale=other[t][:, 0:1])
+            nc.scalar.activation(out=hid[half][:, t, :], in_=src[t][:].indirect(lst[:]), func=COPY, scale=other[t][:, 0:1])
 
-        make_b(0, (0, 1), nc.scalar.copy)
-        make_b(0, (2, 3), nc.scalar.copy)
+        pairs = ((0, 1), (2, 3))
+        for pair in pairs:
+            make_b(0, pair, nc.scalar.copy)
         for t in range(PACK):
             make_a(t)
-            look(0, t)
-        make_b(1, (0, 1), nc.vector.tensor_copy)
-        look(1, 0)
-        look(1, 1)
-        make_b(1, (2, 3), nc.scalar.copy)
-        look(1, 2)
-        look(1, 3)
+            pick(0, t)
+        for pair in pairs:
+            make_b(1, pair, nc.vector.tensor_copy)
+            for t in pair:
+                pick(1, t)
 
-        vsg = gather(vsc, l5, U8, "vsg")
-        vwg = gather(vw, l5, U32, "vwg")
+        vsg = gather(vs_plane, l5, U8, "vsg")
 
         def second_stage(half):
-            woven = sb.tile([P, O, PACK], BF16, name=f"woven{half}", tag="vs_words", align_bytes=64)
+            woven = sb.tile([P, O, PACK], BF16, name=f"woven{half}", tag="vs_bytes", align_bytes=MX_ALIGN)
             nc.vector.tensor_copy(
-                woven[:].rearrange("p (c i) t -> p c t i", i=4), h[half][:].rearrange("p t (c i) -> p c t i", i=4)
+                woven[:].rearrange("p (c i) t -> p c t i", i=RUN), hid[half][:].rearrange("p t (c i) -> p c t i", i=RUN)
             )
-            codes = sb.tile([P, O], U32, name=f"codes{half}", tag=("vs_bytes", "codes1")[half], align_bytes=64)
-            scales = sb.tile([P, O], U8, name=f"scales{half}", align_bytes=64)
+            codes = sb.tile([P, O], U32, name=f"codes{half}", align_bytes=MX_ALIGN)
+            scales = sb.tile([P, O], U8, name=f"scales{half}", align_bytes=MX_ALIGN)
             nc.vector.quantize_mx(out=codes[:].bitcast(E4M3), scales=scales[:], in_=woven[:].rearrange("p d t -> p (d t)"))
-            acc = psum.tile([P, 2, O], F32, name="acc", tag="acc")
-            for i in range(2):
+            acc = psum.tile([P, ROW_TILES, O], F32, name="acc", tag="acc")
+            for i in range(ROW_TILES):
                 cols = slice(P * i, P * (i + 1))
                 nc.tensor.matmul_mx(
                     out=acc[:, i, :], lhsT=vwg[:, cols].bitcast(E5M2), lhsT_scale=vsg[:, cols],
@@ -175,32 +188,18 @@ def tile_list_groupside_ahead_store_pagetwice_kernel(
                 )
             return acc
 
-        p = [sb.tile([P, 2, O], F32, name=f"p{half}") for half in range(2)]
+        accs = [second_stage(half) for half in range(2)]
+        for half in range(2):
+            p_half = sb.tile([P, ROW_TILES, O], F32, name=f"p{half}")
+            nc.scalar.copy(p_half[:], accs[half][:])
+            list_cols = slice(half * O // ENTRIES, (half + 1) * O // ENTRIES)
+            for i in range(ROW_TILES):
+                nc.vector.tensor_copy(pa[i][:].indirect(l6[:, list_cols]), p_half[:, i, :])
+                nc.scalar.activation(out=pb[i][:].indirect(l7[:, list_cols]), in_=p_half[:, i, :], func=COPY)
 
-        def put(engine, page, lst, i, first, count):
-            half, col = divmod(first, O)
-            window = page[i][:].indirect(lst[:, first // 16 : (first + count) // 16])
-            if engine == "vector":
-                nc.vector.tensor_copy(window, p[half][:, i, col : col + count])
-            else:
-                nc.scalar.activation(out=window, in_=p[half][:, i, col : col + count], func=COPY)
-
-        def finish(i):
-            y = sb.tile([P, E], F32, name=f"y{i}")
-            nc.vector.tensor_tensor(y[:], pa[i][:], pb[i][:], ADD)
-            nc.sync.dma_start(out[P * i : P * (i + 1), :], y[:])
-
-        nc.scalar.copy(p[0][:], second_stage(0)[:])
-        late = second_stage(1)
-        put("vector", pa, l6, 0, 0, O)
-        put("scalar", pb, l7, 0, 0, O)
-        nc.vector.tensor_copy(p[1][:], late[:])
-        put("vector", pa, l6, 1, 0, O)
-        put("scalar", pb, l7, 1, 0, O)
-        put("vector", pa, l6, 0, O, O)
-        put("scalar", pb, l7, 0, O, O)
-        put("vector", pa, l6, 1, O, O // 2)
-        put("scalar", pb, l7, 1, O, O)
-        finish(0)
-        put("scalar", pa, l6, 1, O + O // 2, O // 2)
-        finish(1)
+        y = [sb.tile([P, E], F32, name=f"y{i}") for i in range(ROW_TILES)]
+        for i in range(ROW_TILES):
+            for first in range(0, E, PAGE_HALF):
+                cols = slice(first, first + PAGE_HALF)
+                nc.vector.tensor_tensor(y[i][:, cols], pa[i][:, cols], pb[i][:, cols], ADD)
+                nc.sync.dma_start(out[P * i : P * (i + 1), cols], y[i][:, cols])

from contextlib import ExitStack

import concourse.mybir as mybir

K, T, J, R, O, D, N, S, E = 512, 2048, 256, 512, 128, 256, 256, 1024, 512
FLOPS = 2 * K * R * J * 2 + 2 * R * N * D

F32 = mybir.dt.float32
BF16 = mybir.dt.bfloat16
I32 = mybir.dt.int32
U32 = mybir.dt.uint32
U16 = mybir.dt.uint16
U8 = mybir.dt.uint8
E4M3 = mybir.dt.float8_e4m3fn_x4
E5M2 = mybir.dt.float8_e5m2_x4
E2M1 = mybir.dt.float4_e2m1fn_x4
COPY = mybir.ActivationFunctionType.Copy
ADD = mybir.AluOpType.add

P = 128
PACK = 4
QUADS = 4
QUAD_ROWS = P // QUADS
SCALE_ROWS = 4
ENTRIES = 16
LINE = 16
RUN = 4
MX_ALIGN = 64
PSUM_BANKS = 8
SLOT_HALF = J // 2
ROW_TILES = N // P
PAGE_HALF = E // 2


def tile_list_groupside_ahead_store_pagetwice_kernel(
    tc, xt_words, xt_scales, w_words, w_scales, w2_words, w2_scales, vs_words, vs_scales,
    offs, offs2, offs3, offs4, offs5, offs6, offs7, out,
):
    nc = tc.nc
    with ExitStack() as ctx:
        sb = ctx.enter_context(tc.tile_pool(name="sb", bufs=1))
        psum = ctx.enter_context(tc.psum_pool(name="psum", bufs=PSUM_BANKS))

        def load_list(src, name):
            lst = sb.tile(list(src.shape), U16, name=name)
            nc.sync.dma_start(lst[:], src)
            return lst

        def scale_rows(plane, q):
            return plane[QUAD_ROWS * q : QUAD_ROWS * q + SCALE_ROWS, :].bitcast(I32)

        def load_plane(plane, src):
            for q in range(QUADS):
                nc.sync.dma_start(scale_rows(plane, q), src[0, SCALE_ROWS * q : SCALE_ROWS * (q + 1), :].bitcast(I32))

        def words_of(src):
            return src[0].rearrange("p n t -> p (n t)").bitcast(I32)

        def stage_scales(queue, src, name):
            stage = sb.tile([SCALE_ROWS, QUADS, R // 4], I32, name=name)
            queue.dma_start(stage[:], src[0].bitcast(I32).rearrange("(q i) c -> i q c", i=SCALE_ROWS))
            return stage

        def deal(copy, raw, dtype, per_line, name):
            dealt = sb.tile([P, PACK, P], dtype, name=name, align_bytes=MX_ALIGN)
            copy(
                dealt[:].rearrange("p t (c i) -> p c t i", i=per_line),
                raw[:].rearrange("p (c i t) -> p c t i", i=per_line, t=PACK),
            )
            return dealt

        def dealt_scales(stage, plane, name):
            for q in range(QUADS):
                nc.vector.tensor_copy(scale_rows(plane, q), stage[:, q, :])
            return deal(nc.vector.tensor_copy, plane, U8, LINE, name)

        def gather(window, lst, dtype, name):
            picked = sb.tile([P, J], dtype, name=name, align_bytes=MX_ALIGN)
            nc.vector.tensor_copy(picked[:], window[:].indirect(lst[:]))
            return picked

        l2 = load_list(offs2, "l2")
        w2s_stage = stage_scales(nc.scalar, w2_scales, "w2s_stage")
        ws_stage = stage_scales(nc.sync, w_scales, "ws_stage")
        xw = sb.tile([P, T], U32, name="xw")
        nc.scalar.dma_start(xw[:].bitcast(I32), words_of(xt_words))
        xs = sb.tile([P, T], U8, name="xs", tag="xt_bytes", align_bytes=MX_ALIGN)
        nc.gpsimd.memset(xs[:].bitcast(I32), 0)
        load_plane(xs, xt_scales)
        l1 = load_list(offs, "l1")
        w2_raw = sb.tile([P, R], U32, name="w2_raw")
        nc.sync.dma_start(w2_raw[:].bitcast(I32), words_of(w2_words))
        w_raw = sb.tile([P, R], U16, name="w_raw")
        nc.sync.dma_start(w_raw[:].bitcast(I32), w_words[0].bitcast(I32))

        ws_plane = sb.tile([P, R], U8, name="ws_plane")
        w2s_plane = sb.tile([P, R], U8, name="w2s_plane")
        vs_plane = sb.tile([P, S], U8, name="vs_plane", tag="vs_bytes", align_bytes=MX_ALIGN)
        for plane in (ws_plane, w2s_plane, vs_plane):
            nc.vector.memset(plane[:].bitcast(I32), 0)
        pa = [sb.tile([P, E], F32, name=f"pa{i}") for i in range(ROW_TILES)]
        pb = [sb.tile([P, E], F32, name=f"pb{i}") for i in range(ROW_TILES)]
        for page in pa + pb:
            nc.vector.memset(page[:], 0.0)

        vw = sb.tile([P, S], U32, name="vw", tag="vs_words", align_bytes=MX_ALIGN)
        nc.sync.dma_start(vw[:].bitcast(I32), words_of(vs_words))
        l5 = load_list(offs5, "l5")
        l3 = load_list(offs3, "l3")
        l4 = load_list(offs4, "l4")
        load_plane(vs_plane, vs_scales)
        l6 = load_list(offs6, "l6")
        l7 = load_list(offs7, "l7")

        w2s = dealt_scales(w2s_stage, w2s_plane, "w2s")
        ws = dealt_scales(ws_stage, ws_plane, "ws")
        xs2 = gather(xs, l2, U8, "xs2")
        xs1 = gather(xs, l1, U8, "xs1")
        w2 = deal(nc.scalar.copy, w2_raw, U32, LINE // 4, "w2")
        w = deal(nc.scalar.copy, w_raw, U16, LINE // 2, "w")
        xw2 = sb.tile([P, J], U32, name="xw2", tag="xt_bytes", align_bytes=MX_ALIGN)

        def gather_xw2(part):
            first, last = SLOT_HALF * part, SLOT_HALF * (part + 1)
            nc.vector.tensor_copy(xw2[:, first:last], xw[:].indirect(l2[:, first // ENTRIES : last // ENTRIES]))

        gather_xw2(0)
        xw1 = gather(xw, l1, U32, "xw1")
        gather_xw2(1)

        vwg = gather(vw, l5, U32, "vwg")
        a = [
            sb.tile([P, J], F32, name=f"a{t}", tag=f"a{t}" if t else "vs_words", align_bytes=MX_ALIGN) for t in range(PACK)
        ]
        b = [sb.tile([P, J], F32, name=f"b{t}") for t in range(PACK)]
        hid = [sb.tile([P, PACK, O], BF16, name=f"hid{half}") for half in range(2)]

        def make_a(t):
            acc = psum.tile([P, J], F32, name="acc", tag="acc")
            nc.tensor.matmul_mx(
                out=acc[:], lhsT=w[:, t, :].bitcast(E2M1), lhsT_scale=ws[:, t, :],
                rhs=xw1[:].bitcast(E4M3), rhs_scale=xs1[:], start=True, stop=True,
            )
            nc.vector.tensor_copy(a[t][:], acc[:])

        def make_b(part, pair, copy):
            cols = slice(SLOT_HALF * part, SLOT_HALF * (part + 1))
            acc = psum.tile([P, len(pair), SLOT_HALF], F32, name="acc", tag="acc")
            for n, t in enumerate(pair):
                nc.tensor.matmul_mx(
                    out=acc[:, n, :], lhsT=w2[:, t, :].bitcast(E5M2), lhsT_scale=w2s[:, t, :],
                    rhs=xw2[:, cols].bitcast(E4M3), rhs_scale=xs2[:, cols], start=True, stop=True,
                )
            for n, t in enumerate(pair):
                copy(b[t][:, cols], acc[:, n, :])

        def pick(half, t):
            src, lst, other = ((a, l3, b), (b, l4, a))[half]
            nc.scalar.activation(out=hid[half][:, t, :], in_=src[t][:].indirect(lst[:]), func=COPY, scale=other[t][:, 0:1])

        pairs = ((0, 1), (2, 3))
        for pair in pairs:
            make_b(0, pair, nc.scalar.copy)
        for t in range(PACK):
            make_a(t)
            pick(0, t)
        for pair in pairs:
            make_b(1, pair, nc.vector.tensor_copy)
            for t in pair:
                pick(1, t)

        vsg = gather(vs_plane, l5, U8, "vsg")

        def second_stage(half):
            woven = sb.tile([P, O, PACK], BF16, name=f"woven{half}", tag="vs_bytes", align_bytes=MX_ALIGN)
            nc.vector.tensor_copy(
                woven[:].rearrange("p (c i) t -> p c t i", i=RUN), hid[half][:].rearrange("p t (c i) -> p c t i", i=RUN)
            )
            codes = sb.tile([P, O], U32, name=f"codes{half}", align_bytes=MX_ALIGN)
            scales = sb.tile([P, O], U8, name=f"scales{half}", align_bytes=MX_ALIGN)
            nc.vector.quantize_mx(out=codes[:].bitcast(E4M3), scales=scales[:], in_=woven[:].rearrange("p d t -> p (d t)"))
            acc = psum.tile([P, ROW_TILES, O], F32, name="acc", tag="acc")
            for i in range(ROW_TILES):
                cols = slice(P * i, P * (i + 1))
                nc.tensor.matmul_mx(
                    out=acc[:, i, :], lhsT=vwg[:, cols].bitcast(E5M2), lhsT_scale=vsg[:, cols],
                    rhs=codes[:].bitcast(E4M3), rhs_scale=scales[:], start=True, stop=True,
                )
            return acc

        accs = [second_stage(half) for half in range(2)]
        for half in range(2):
            p_half = sb.tile([P, ROW_TILES, O], F32, name=f"p{half}")
            nc.scalar.copy(p_half[:], accs[half][:])
            list_cols = slice(half * O // ENTRIES, (half + 1) * O // ENTRIES)
            for i in range(ROW_TILES):
                nc.vector.tensor_copy(pa[i][:].indirect(l6[:, list_cols]), p_half[:, i, :])
                nc.scalar.activation(out=pb[i][:].indirect(l7[:, list_cols]), in_=p_half[:, i, :], func=COPY)

        y = [sb.tile([P, E], F32, name=f"y{i}") for i in range(ROW_TILES)]
        for i in range(ROW_TILES):
            for first in range(0, E, PAGE_HALF):
                cols = slice(first, first + PAGE_HALF)
                nc.vector.tensor_tensor(y[i][:, cols], pa[i][:, cols], pb[i][:, cols], ADD)
                nc.sync.dma_start(out[P * i : P * (i + 1), cols], y[i][:, cols])
